import numpy as np
import ml_dtypes


def mxq(x, axis, fmt="e4m3"):
    dtype, down = {"e4m3": (ml_dtypes.float8_e4m3fn, 7), "e5m2": (ml_dtypes.float8_e5m2, 14)}[fmt]
    v = np.moveaxis(np.asarray(x, np.float32).astype(ml_dtypes.bfloat16).astype(np.float64), axis, -1)
    blocks = v.reshape(v.shape[:-1] + (-1, 32))
    amax = np.abs(blocks).max(-1, keepdims=True)
    byte = np.maximum(np.where(amax > 0, np.frexp(amax)[1] - 1 + 127, 0) - down, 1)
    scale = np.exp2(byte - 127.0)
    codes = (blocks / scale).astype(np.float32).astype(dtype).astype(np.float64)
    return np.moveaxis((codes * scale).reshape(v.shape), -1, axis)


WIDE = False


def mx_kscale(k):
    if not WIDE:
        return np.ones(k)
    levels = np.array([10, -10, 5, -5, 0])
    if k % 512:
        return np.exp2(np.random.permutation(np.resize(levels, k // 32))).repeat(32)
    a = np.empty((k // 512, 16))
    for p in range(k // 512):
        a[p, :8] = np.random.permutation(np.resize(levels, 8))
        for g in range(8):
            far = levels[np.abs(levels - a[p, g]) >= 10]
            a[p, g + 8] = far[np.random.randint(len(far))]
    return np.exp2(a.ravel()).repeat(32)


def f64(x):
    return np.asarray(x).astype(np.float64)


def striped8(idx):
    return np.asarray(idx).reshape(8, -1, 16).transpose(0, 2, 1).reshape(128, -1).astype(np.uint16)


def unstriped8(offs):
    return offs.reshape(8, 16, -1).transpose(0, 2, 1).reshape(8, -1).astype(np.int64)


def pick8(x, idx, run):
    r = np.arange(len(x))
    return x[r[:, None], idx[r % (8 * run) // run]]


E2M1 = np.array([0.0, 0.5, 1.0, 1.5, 2.0, 3.0, 4.0, 6.0, -0.0, -0.5, -1.0, -1.5, -2.0, -3.0, -4.0, -6.0])


def pack_weight(w, fmt):
    k, n = w.shape
    w = f64(np.asarray(w, np.float32).astype(ml_dtypes.bfloat16)).reshape(k // 32, 32, n)
    amax = np.abs(w).max(1)
    if fmt == "e4m3":
        byte = np.frexp(amax)[1] - 1 + 127 - 7
    else:
        mant, ex = np.frexp(amax / 6.0)
        byte = np.where(mant > 0.5, ex, ex - 1) + 127
    byte = np.clip(np.where(amax > 0, byte, 1), 1, 254)
    scaled = (w * np.exp2(127.0 - byte)[:, None, :]).reshape(k, n).astype(np.float32)
    by_word = np.ascontiguousarray(scaled.reshape(k // 512, 128, 4, n).transpose(0, 1, 3, 2))
    if fmt == "e4m3":
        words = by_word.astype(ml_dtypes.float8_e4m3fn).view(np.uint8)
    else:
        c = by_word.astype(ml_dtypes.float4_e2m1fn).view(np.uint8) & 0xF
        words = (c[..., 0::2] | (c[..., 1::2] << 4)).reshape(k // 512, 128, 2 * n)
    return np.ascontiguousarray(words), np.ascontiguousarray(byte.astype(np.uint8).reshape(k // 512, 16, n))


def unpack_weight(words, scales, fmt):
    g, _, n = scales.shape
    words = np.ascontiguousarray(words).reshape(g, 128, n, -1)
    if fmt == "e4m3":
        vals = words.view(ml_dtypes.float8_e4m3fn).astype(np.float64)
    else:
        nib = np.empty((g, 128, n, 4), np.uint8)
        nib[..., 0::2] = words & 0xF
        nib[..., 1::2] = words >> 4
        vals = E2M1[nib]
    vals = vals * np.repeat(np.exp2(scales.astype(np.float64) - 127.0), 8, axis=1)[..., None]
    return vals.transpose(0, 1, 3, 2).reshape(g * 512, n)


D, T, U, X, I, Q = 512, 1024, 1024, 1024, 512, 128


def setup_inputs():
    n = np.random.standard_normal
    idx = np.stack([np.random.permutation(T)[:I] for _ in range(8)])
    idx2 = np.stack([np.random.permutation(U)[:I] for _ in range(8)])
    idx3 = np.stack([np.random.permutation(X)[:I] for _ in range(8)])
    idx4 = np.stack([np.random.permutation(U)[:I] for _ in range(8)])
    idx5 = np.stack([np.random.permutation(X)[:I] for _ in range(8)])
    idx6 = np.stack([np.random.permutation(T)[:I] for _ in range(8)])
    fd = mx_kscale(D)
    keysp = pack_weight(n((D, T)) / fd[:, None], "e4m3")
    notesp = pack_weight(n((D, U)) / fd[:, None], "e2m1")
    usersp = pack_weight(n((D, X)) / fd[:, None], "e4m3")
    return {
        "query": (n((D, Q)) * 1.0 / np.sqrt(D) * fd[:, None]).astype(np.float32),
        "keys_words": keysp[0],
        "keys_scales": keysp[1],
        "notes_words": notesp[0],
        "notes_scales": notesp[1],
        "users_words": usersp[0],
        "users_scales": usersp[1],
        "offs": striped8(idx),
        "offs2": striped8(idx2),
        "offs3": striped8(idx3),
        "offs4": striped8(idx4),
        "offs5": striped8(idx5),
        "offs6": striped8(idx6),
    }


def reference(query, keys_words, keys_scales, notes_words, notes_scales, users_words, users_scales, offs, offs2, offs3, offs4, offs5, offs6):
    idx = unstriped8(offs)
    idx2 = unstriped8(offs2)
    idx3 = unstriped8(offs3)
    idx4 = unstriped8(offs4)
    idx5 = unstriped8(offs5)
    idx6 = unstriped8(offs6)
    keysu = unpack_weight(keys_words, keys_scales, "e4m3")
    notesu = unpack_weight(notes_words, notes_scales, "e2m1")
    usersu = unpack_weight(users_words, users_scales, "e4m3")
    queryq = mxq(f64(query), 0, "e4m3")
    a = queryq.T @ keysu
    b = queryq.T @ notesu
    c0 = queryq.T @ usersu
    f1 = np.zeros((Q, U))
    f1[np.arange(Q)[:, None], idx2[np.arange(Q) % 128 // 16]] = pick8(a, idx, 16)
    f2 = np.zeros((Q, X))
    f2[np.arange(Q)[:, None], idx3[np.arange(Q) % 128 // 16]] = pick8(a, idx, 16)
    bb = b + f1
    cc = c0 - f2
    w = np.minimum(pick8(bb, idx4, 16), pick8(cc, idx5, 16))
    f3 = np.zeros((Q, T))
    f3[np.arange(Q)[:, None], idx6[np.arange(Q) % 128 // 16]] = w
    aa = a - f3
    y = pick8(aa, idx, 16) + w
    return y

@@ -1,0 +1,152 @@
+from contextlib import ExitStack
+
+import concourse.mybir as mybir
+
+F32 = mybir.dt.float32
+BF16 = mybir.dt.bfloat16
+I32 = mybir.dt.int32
+U32 = mybir.dt.uint32
+U16 = mybir.dt.uint16
+U8 = mybir.dt.uint8
+FP8X4 = mybir.dt.float8_e4m3fn_x4
+FP4X4 = mybir.dt.float4_e2m1fn_x4
+ALU = mybir.AluOpType
+COPY = mybir.ActivationFunctionType.Copy
+
+P = 128
+PACK = 4
+Q = 128
+POOL = 1024
+SLOTS = 512
+HALF = SLOTS // 2
+LCOLS = SLOTS // 16
+BANK = 512
+FLOPS = 3 * 2 * 512 * Q * POOL
+
+
+def tile_attend_mergeback_three_kernel(tc, query, keys_words, keys_scales, notes_words, notes_scales,
+                                        users_words, users_scales, offs, offs2, offs3, offs4, offs5, offs6, out):
+    nc = tc.nc
+    with ExitStack() as ctx:
+        sb = ctx.enter_context(tc.tile_pool(name="sb", bufs=1))
+        ps = ctx.enter_context(tc.psum_pool(name="ps", bufs=1))
+
+        def load_list(src, name):
+            t = sb.tile([P, LCOLS], U16, name=name)
+            nc.sync.dma_start(t[:], src)
+            return t
+
+        def zeroed_plane(name):
+            t = sb.tile([P, POOL], U8, name=name, align_bytes=64)
+            nc.vector.memset(t[:].bitcast(I32), 0)
+            return t
+
+        def load_plane(queue, plane, src):
+            for g in range(4):
+                queue.dma_start(plane[32 * g:32 * g + 4, :].bitcast(I32), src[0, 4 * g:4 * g + 4, :].bitcast(I32))
+
+        def half(lst, h):
+            return lst[:, h * (LCOLS // 2):(h + 1) * (LCOLS // 2)]
+
+        def cols(h):
+            return slice(h * HALF, (h + 1) * HALF)
+
+        k_scale = zeroed_plane("k_scale")
+        q_raw = sb.tile([P, PACK, Q], F32, name="q_raw")
+        nc.sync.dma_start(q_raw[:], query.rearrange("(p j) q -> p j q", j=PACK))
+        k_flat = keys_words[0].rearrange("p n t -> p (n t)")
+        k_words = []
+        for h in range(2):
+            t = sb.tile([P, BANK], U32, name="k_words%d" % h, align_bytes=64)
+            k_words.append(t)
+        nc.sync.dma_start(k_words[0][:].bitcast(I32), k_flat[:, 0:4 * BANK].bitcast(I32))
+        l1 = load_list(offs, "l1")
+        load_plane(nc.scalar, k_scale, keys_scales)
+        nc.scalar.dma_start(k_words[1][:].bitcast(I32), k_flat[:, 4 * BANK:8 * BANK].bitcast(I32))
+
+        n_scale = zeroed_plane("n_scale")
+        u_scale = zeroed_plane("u_scale")
+        f1 = sb.tile([P, POOL], F32, name="f1")
+        nc.vector.memset(f1[:].bitcast(I32), 0)
+        f2 = sb.tile([P, POOL], F32, name="f2")
+        nc.vector.memset(f2[:].bitcast(I32), 0)
+
+        l2 = load_list(offs2, "l2")
+        l3 = load_list(offs3, "l3")
+        n_words = sb.tile([P, 2 * POOL], U8, name="n_words", align_bytes=64)
+        nc.sync.dma_start(n_words[:].bitcast(I32), notes_words[0].bitcast(I32))
+        load_plane(nc.sync, n_scale, notes_scales)
+        u_words = sb.tile([P, POOL], U32, name="u_words", align_bytes=64)
+        nc.sync.dma_start(u_words[:].bitcast(I32), users_words[0].rearrange("p n t -> p (n t)").bitcast(I32))
+        load_plane(nc.sync, u_scale, users_scales)
+        l4 = load_list(offs4, "l4")
+        l5 = load_list(offs5, "l5")
+        l6 = load_list(offs6, "l6")
+
+        q_bf = sb.tile([P, Q, PACK], BF16, name="q_bf", tag="late_zero", align_bytes=64)
+        q_codes = sb.tile([P, Q], U32, name="q_codes", align_bytes=64)
+        q_scale = sb.tile([P, Q], U8, name="q_scale", align_bytes=64)
+        for h in range(2):
+            s = slice(64 * h, 64 * h + 64)
+            nc.vector.tensor_copy(out=q_bf[:, s, :].rearrange("p (c i) t -> p c t i", i=4),
+                                  in_=q_raw[:, :, s].rearrange("p t (c i) -> p c t i", i=4))
+        for h in range(2):
+            s = slice(64 * h, 64 * h + 64)
+            nc.vector.quantize_mx(out=q_codes[:, s].bitcast(FP8X4), scales=q_scale[:, s],
+                                  in_=q_bf[:, s, :].rearrange("p q t -> p (q t)"))
+        f3 = sb.tile([P, POOL], F32, name="f3", tag="late_zero", align_bytes=64)
+        nc.vector.memset(f3[:].bitcast(I32), 0)
+
+        def scores(name, words, scales):
+            acc = ps.tile([P, scales.shape[1]], F32, name=name)
+            nc.tensor.matmul_mx(out=acc[:], lhsT=q_codes[:].bitcast(FP8X4), lhsT_scale=q_scale[:],
+                                rhs=words, rhs_scale=scales, start=True, stop=True)
+            return acc
+
+        a_sb = sb.tile([P, POOL], F32, name="a_sb")
+        a0 = scores("a0", k_words[0][:].bitcast(FP8X4), k_scale[:, 0:512])
+        a1 = scores("a1", k_words[1][:, 0:256].bitcast(FP8X4), k_scale[:, 512:768])
+        a2 = scores("a2", k_words[1][:, 256:512].bitcast(FP8X4), k_scale[:, 768:1024])
+        nc.scalar.activation(a_sb[:, 0:512], a0[:], COPY)
+        nc.vector.tensor_copy(a_sb[:, 512:768], a1[:])
+        nc.vector.tensor_copy(a_sb[:, 768:1024], a2[:])
+        b = [scores("b%d" % h, n_words[:, h * 2 * BANK:(h + 1) * 2 * BANK].bitcast(FP4X4),
+                    n_scale[:, h * BANK:(h + 1) * BANK]) for h in range(2)]
+        c = [scores("c%d" % h, u_words[:, h * BANK:(h + 1) * BANK].bitcast(FP8X4),
+                    u_scale[:, h * BANK:(h + 1) * BANK]) for h in range(2)]
+
+        g = sb.tile([P, SLOTS], F32, name="g")
+        nc.vector.tensor_copy(g[:, cols(0)], a_sb[:].indirect(half(l1, 0)))
+        nc.scalar.activation(g[:, cols(1)], a_sb[:].indirect(half(l1, 1)), COPY)
+        for h in range(2):
+            nc.vector.tensor_copy(f1[:].indirect(half(l2, h)), g[:, cols(h)])
+        nc.vector.tensor_copy(f2[:].indirect(l3[:]), g[:])
+
+        bb = sb.tile([P, POOL], F32, name="bb")
+        cc = sb.tile([P, POOL], F32, name="cc")
+        for h in range(2):
+            s = slice(h * BANK, (h + 1) * BANK)
+            nc.vector.tensor_tensor(bb[:, s], b[h][:], f1[:, s], ALU.add)
+        for h in range(2):
+            s = slice(h * BANK, (h + 1) * BANK)
+            nc.vector.tensor_tensor(cc[:, s], c[h][:], f2[:, s], ALU.subtract)
+        gb = sb.tile([P, SLOTS], F32, name="gb")
+        gc = sb.tile([P, SLOTS], F32, name="gc")
+        w = sb.tile([P, SLOTS], F32, name="w")
+        nc.scalar.activation(gb[:], bb[:].indirect(l4[:]), COPY)
+        nc.vector.tensor_copy(gc[:, cols(0)], cc[:].indirect(half(l5, 0)))
+        nc.scalar.activation(gc[:, cols(1)], cc[:].indirect(half(l5, 1)), COPY)
+        for h in range(2):
+            nc.vector.tensor_tensor(w[:, cols(h)], gb[:, cols(h)], gc[:, cols(h)], ALU.min)
+        for h in range(2):
+            nc.vector.tensor_copy(f3[:].indirect(half(l6, h)), w[:, cols(h)])
+
+        aa = sb.tile([P, POOL], F32, name="aa")
+        nc.vector.tensor_tensor(aa[:], a_sb[:], f3[:], ALU.subtract)
+        y = sb.tile([P, SLOTS], F32, name="y")
+        ga = sb.tile([P, HALF], F32, name="ga")
+        nc.vector.tensor_tensor(y[:, cols(0)], aa[:].indirect(half(l1, 0)), w[:, cols(0)], ALU.add)
+        nc.scalar.activation(ga[:], aa[:].indirect(half(l1, 1)), COPY)
+        nc.sync.dma_start(out[:, cols(0)], y[:, cols(0)])
+        nc.vector.tensor_tensor(y[:, cols(1)], ga[:], w[:, cols(1)], ALU.add)
+        nc.sync.dma_start(out[:, cols(1)], y[:, cols(1)])

@@ -21,6 +21,7 @@ SLOTS = 512
 HALF = SLOTS // 2
 LCOLS = SLOTS // 16
 BANK = 512
+SPLIT = 704
 FLOPS = 3 * 2 * 512 * Q * POOL
 
 
@@ -38,11 +39,10 @@ def tile_attend_mergeback_three_kernel(tc, query, keys_words, keys_scales, notes
 
         def zeroed_plane(name):
             t = sb.tile([P, POOL], U8, name=name, align_bytes=64)
-            nc.vector.memset(t[:].bitcast(I32), 0)
             return t
 
-        def load_plane(queue, plane, src):
-            for g in range(4):
+        def load_plane(queues, plane, src):
+            for g, queue in enumerate(queues):
                 queue.dma_start(plane[32 * g:32 * g + 4, :].bitcast(I32), src[0, 4 * g:4 * g + 4, :].bitcast(I32))
 
         def half(lst, h):
@@ -59,10 +59,10 @@ def tile_attend_mergeback_three_kernel(tc, query, keys_words, keys_scales, notes
         for h in range(2):
             t = sb.tile([P, BANK], U32, name="k_words%d" % h, align_bytes=64)
             k_words.append(t)
-        nc.sync.dma_start(k_words[0][:].bitcast(I32), k_flat[:, 0:4 * BANK].bitcast(I32))
+        load_plane([nc.scalar, nc.sync, nc.scalar, nc.scalar], k_scale, keys_scales)
+        for h in range(2):
+            nc.sync.dma_start(k_words[h][:].bitcast(I32), k_flat[:, h * 4 * BANK:(h + 1) * 4 * BANK].bitcast(I32))
         l1 = load_list(offs, "l1")
-        load_plane(nc.scalar, k_scale, keys_scales)
-        nc.scalar.dma_start(k_words[1][:].bitcast(I32), k_flat[:, 4 * BANK:8 * BANK].bitcast(I32))
 
         n_scale = zeroed_plane("n_scale")
         u_scale = zeroed_plane("u_scale")
@@ -72,13 +72,13 @@ def tile_attend_mergeback_three_kernel(tc, query, keys_words, keys_scales, notes
         nc.vector.memset(f2[:].bitcast(I32), 0)
 
         l2 = load_list(offs2, "l2")
-        l3 = load_list(offs3, "l3")
         n_words = sb.tile([P, 2 * POOL], U8, name="n_words", align_bytes=64)
         nc.sync.dma_start(n_words[:].bitcast(I32), notes_words[0].bitcast(I32))
-        load_plane(nc.sync, n_scale, notes_scales)
+        load_plane([nc.sync] * 4, n_scale, notes_scales)
+        l3 = load_list(offs3, "l3")
         u_words = sb.tile([P, POOL], U32, name="u_words", align_bytes=64)
         nc.sync.dma_start(u_words[:].bitcast(I32), users_words[0].rearrange("p n t -> p (n t)").bitcast(I32))
-        load_plane(nc.sync, u_scale, users_scales)
+        load_plane([nc.sync] * 4, u_scale, users_scales)
         l4 = load_list(offs4, "l4")
         l5 = load_list(offs5, "l5")
         l6 = load_list(offs6, "l6")
@@ -106,10 +106,12 @@ def tile_attend_mergeback_three_kernel(tc, query, keys_words, keys_scales, notes
         a_sb = sb.tile([P, POOL], F32, name="a_sb")
         a0 = scores("a0", k_words[0][:].bitcast(FP8X4), k_scale[:, 0:512])
         a1 = scores("a1", k_words[1][:, 0:256].bitcast(FP8X4), k_scale[:, 512:768])
-        a2 = scores("a2", k_words[1][:, 256:512].bitcast(FP8X4), k_scale[:, 768:1024])
+        a2 = scores("a2", k_words[1][:, 256:384].bitcast(FP8X4), k_scale[:, 768:896])
+        a3 = scores("a3", k_words[1][:, 384:512].bitcast(FP8X4), k_scale[:, 896:1024])
         nc.scalar.activation(a_sb[:, 0:512], a0[:], COPY)
         nc.vector.tensor_copy(a_sb[:, 512:768], a1[:])
-        nc.vector.tensor_copy(a_sb[:, 768:1024], a2[:])
+        nc.vector.tensor_copy(a_sb[:, 768:896], a2[:])
+        nc.scalar.activation(a_sb[:, 896:1024], a3[:], COPY)
         b = [scores("b%d" % h, n_words[:, h * 2 * BANK:(h + 1) * 2 * BANK].bitcast(FP4X4),
                     n_scale[:, h * BANK:(h + 1) * BANK]) for h in range(2)]
         c = [scores("c%d" % h, u_words[:, h * BANK:(h + 1) * BANK].bitcast(FP8X4),
@@ -118,31 +120,34 @@ def tile_attend_mergeback_three_kernel(tc, query, keys_words, keys_scales, notes
         g = sb.tile([P, SLOTS], F32, name="g")
         nc.vector.tensor_copy(g[:, cols(0)], a_sb[:].indirect(half(l1, 0)))
         nc.scalar.activation(g[:, cols(1)], a_sb[:].indirect(half(l1, 1)), COPY)
-        for h in range(2):
-            nc.vector.tensor_copy(f1[:].indirect(half(l2, h)), g[:, cols(h)])
+        nc.vector.tensor_copy(f1[:].indirect(l2[:]), g[:])
         nc.vector.tensor_copy(f2[:].indirect(l3[:]), g[:])
 
-        bb = sb.tile([P, POOL], F32, name="bb")
+        bb = sb.tile([P, POOL], F32, name="bb", tag="bb_then_gc")
         cc = sb.tile([P, POOL], F32, name="cc")
+        b_sb = sb.tile([P, POOL], F32, name="b_sb")
         for h in range(2):
-            s = slice(h * BANK, (h + 1) * BANK)
-            nc.vector.tensor_tensor(bb[:, s], b[h][:], f1[:, s], ALU.add)
-        for h in range(2):
-            s = slice(h * BANK, (h + 1) * BANK)
-            nc.vector.tensor_tensor(cc[:, s], c[h][:], f2[:, s], ALU.subtract)
+            nc.scalar.copy(b_sb[:, h * BANK:(h + 1) * BANK], b[h][:])
+        c_sb = sb.tile([P, POOL - SPLIT], F32, name="c_sb")
+        nc.scalar.copy(c_sb[:], c[1][:, SPLIT - BANK:])
+        nc.gpsimd.tensor_tensor(bb[:], b_sb[:], f1[:], ALU.add)
+        nc.vector.tensor_tensor(cc[:, :BANK], c[0][:], f2[:, :BANK], ALU.subtract)
+        nc.vector.tensor_tensor(cc[:, BANK:SPLIT], c[1][:, :SPLIT - BANK], f2[:, BANK:SPLIT], ALU.subtract)
+        nc.gpsimd.tensor_tensor(cc[:, SPLIT:], c_sb[:], f2[:, SPLIT:], ALU.subtract)
         gb = sb.tile([P, SLOTS], F32, name="gb")
-        gc = sb.tile([P, SLOTS], F32, name="gc")
         w = sb.tile([P, SLOTS], F32, name="w")
         nc.scalar.activation(gb[:], bb[:].indirect(l4[:]), COPY)
-        nc.vector.tensor_copy(gc[:, cols(0)], cc[:].indirect(half(l5, 0)))
-        nc.scalar.activation(gc[:, cols(1)], cc[:].indirect(half(l5, 1)), COPY)
+        gc = [sb.tile([P, HALF], F32, name="gc0"), sb.tile([P, HALF], F32, name="gc1", tag="bb_then_gc")]
+        nc.vector.tensor_copy(gc[0][:], cc[:].indirect(half(l5, 0)))
+        nc.scalar.activation(gc[1][:], cc[:].indirect(half(l5, 1)), COPY)
         for h in range(2):
-            nc.vector.tensor_tensor(w[:, cols(h)], gb[:, cols(h)], gc[:, cols(h)], ALU.min)
-        for h in range(2):
-            nc.vector.tensor_copy(f3[:].indirect(half(l6, h)), w[:, cols(h)])
+            nc.vector.tensor_tensor(w[:, cols(h)], gb[:, cols(h)], gc[h][:], ALU.min)
+        nc.vector.tensor_copy(f3[:].indirect(l6[:]), w[:])
 
         aa = sb.tile([P, POOL], F32, name="aa")
-        nc.vector.tensor_tensor(aa[:], a_sb[:], f3[:], ALU.subtract)
+        nc.vector.tensor_tensor(aa[:, :BANK], a0[:], f3[:, :BANK], ALU.subtract)
+        nc.vector.tensor_tensor(aa[:, BANK:SPLIT], a1[:, :SPLIT - BANK], f3[:, BANK:SPLIT], ALU.subtract)
+        nc.gpsimd.tensor_tensor(aa[:, SPLIT:], a_sb[:, SPLIT:], f3[:, SPLIT:], ALU.subtract)
         y = sb.tile([P, SLOTS], F32, name="y")
         ga = sb.tile([P, HALF], F32, name="ga")
         nc.vector.tensor_tensor(y[:, cols(0)], aa[:].indirect(half(l1, 0)), w[:, cols(0)], ALU.add)

@@ -21,7 +21,6 @@ SLOTS = 512
 HALF = SLOTS // 2
 LCOLS = SLOTS // 16
 BANK = 512
-SPLIT = 704
 FLOPS = 3 * 2 * 512 * Q * POOL
 
 
@@ -128,12 +127,10 @@ def tile_attend_mergeback_three_kernel(tc, query, keys_words, keys_scales, notes
         b_sb = sb.tile([P, POOL], F32, name="b_sb")
         for h in range(2):
             nc.scalar.copy(b_sb[:, h * BANK:(h + 1) * BANK], b[h][:])
-        c_sb = sb.tile([P, POOL - SPLIT], F32, name="c_sb")
-        nc.scalar.copy(c_sb[:], c[1][:, SPLIT - BANK:])
         nc.gpsimd.tensor_tensor(bb[:], b_sb[:], f1[:], ALU.add)
-        nc.vector.tensor_tensor(cc[:, :BANK], c[0][:], f2[:, :BANK], ALU.subtract)
-        nc.vector.tensor_tensor(cc[:, BANK:SPLIT], c[1][:, :SPLIT - BANK], f2[:, BANK:SPLIT], ALU.subtract)
-        nc.gpsimd.tensor_tensor(cc[:, SPLIT:], c_sb[:], f2[:, SPLIT:], ALU.subtract)
+        for h in range(2):
+            s = slice(h * BANK, (h + 1) * BANK)
+            nc.vector.tensor_tensor(cc[:, s], c[h][:], f2[:, s], ALU.subtract)
         gb = sb.tile([P, SLOTS], F32, name="gb")
         w = sb.tile([P, SLOTS], F32, name="w")
         nc.scalar.activation(gb[:], bb[:].indirect(l4[:]), COPY)
@@ -145,9 +142,7 @@ def tile_attend_mergeback_three_kernel(tc, query, keys_words, keys_scales, notes
         nc.vector.tensor_copy(f3[:].indirect(l6[:]), w[:])
 
         aa = sb.tile([P, POOL], F32, name="aa")
-        nc.vector.tensor_tensor(aa[:, :BANK], a0[:], f3[:, :BANK], ALU.subtract)
-        nc.vector.tensor_tensor(aa[:, BANK:SPLIT], a1[:, :SPLIT - BANK], f3[:, BANK:SPLIT], ALU.subtract)
-        nc.gpsimd.tensor_tensor(aa[:, SPLIT:], a_sb[:, SPLIT:], f3[:, SPLIT:], ALU.subtract)
+        nc.vector.tensor_tensor(aa[:], a_sb[:], f3[:], ALU.subtract)
         y = sb.tile([P, SLOTS], F32, name="y")
         ga = sb.tile([P, HALF], F32, name="ga")
         nc.vector.tensor_tensor(y[:, cols(0)], aa[:].indirect(half(l1, 0)), w[:, cols(0)], ALU.add)

@@ -144,9 +144,6 @@ def tile_attend_mergeback_three_kernel(tc, query, keys_words, keys_scales, notes
         aa = sb.tile([P, POOL], F32, name="aa")
         nc.vector.tensor_tensor(aa[:], a_sb[:], f3[:], ALU.subtract)
         y = sb.tile([P, SLOTS], F32, name="y")
-        ga = sb.tile([P, HALF], F32, name="ga")
-        nc.vector.tensor_tensor(y[:, cols(0)], aa[:].indirect(half(l1, 0)), w[:, cols(0)], ALU.add)
-        nc.scalar.activation(ga[:], aa[:].indirect(half(l1, 1)), COPY)
-        nc.sync.dma_start(out[:, cols(0)], y[:, cols(0)])
-        nc.vector.tensor_tensor(y[:, cols(1)], ga[:], w[:, cols(1)], ALU.add)
-        nc.sync.dma_start(out[:, cols(1)], y[:, cols(1)])
+        for h in range(2):
+            nc.vector.tensor_tensor(y[:, cols(h)], aa[:].indirect(half(l1, h)), w[:, cols(h)], ALU.add)
+            nc.sync.dma_start(out[:, cols(h)], y[:, cols(h)])

from contextlib import ExitStack

import concourse.mybir as mybir

F32 = mybir.dt.float32
BF16 = mybir.dt.bfloat16
I32 = mybir.dt.int32
U32 = mybir.dt.uint32
U16 = mybir.dt.uint16
U8 = mybir.dt.uint8
FP8X4 = mybir.dt.float8_e4m3fn_x4
FP4X4 = mybir.dt.float4_e2m1fn_x4
ALU = mybir.AluOpType
COPY = mybir.ActivationFunctionType.Copy

P = 128
PACK = 4
Q = 128
POOL = 1024
SLOTS = 512
HALF = SLOTS // 2
LCOLS = SLOTS // 16
BANK = 512
FLOPS = 3 * 2 * 512 * Q * POOL


def tile_attend_mergeback_three_kernel(tc, query, keys_words, keys_scales, notes_words, notes_scales,
                                        users_words, users_scales, offs, offs2, offs3, offs4, offs5, offs6, out):
    nc = tc.nc
    with ExitStack() as ctx:
        sb = ctx.enter_context(tc.tile_pool(name="sb", bufs=1))
        ps = ctx.enter_context(tc.psum_pool(name="ps", bufs=1))

        def load_list(src, name):
            t = sb.tile([P, LCOLS], U16, name=name)
            nc.sync.dma_start(t[:], src)
            return t

        def zeroed_plane(name):
            t = sb.tile([P, POOL], U8, name=name, align_bytes=64)
            return t

        def load_plane(queues, plane, src):
            for g, queue in enumerate(queues):
                queue.dma_start(plane[32 * g:32 * g + 4, :].bitcast(I32), src[0, 4 * g:4 * g + 4, :].bitcast(I32))

        def half(lst, h):
            return lst[:, h * (LCOLS // 2):(h + 1) * (LCOLS // 2)]

        def cols(h):
            return slice(h * HALF, (h + 1) * HALF)

        k_scale = zeroed_plane("k_scale")
        q_raw = sb.tile([P, PACK, Q], F32, name="q_raw")
        nc.sync.dma_start(q_raw[:], query.rearrange("(p j) q -> p j q", j=PACK))
        k_flat = keys_words[0].rearrange("p n t -> p (n t)")
        k_words = []
        for h in range(2):
            t = sb.tile([P, BANK], U32, name="k_words%d" % h, align_bytes=64)
            k_words.append(t)
        load_plane([nc.scalar, nc.sync, nc.scalar, nc.scalar], k_scale, keys_scales)
        for h in range(2):
            nc.sync.dma_start(k_words[h][:].bitcast(I32), k_flat[:, h * 4 * BANK:(h + 1) * 4 * BANK].bitcast(I32))
        l1 = load_list(offs, "l1")

        n_scale = zeroed_plane("n_scale")
        u_scale = zeroed_plane("u_scale")
        f1 = sb.tile([P, POOL], F32, name="f1")
        nc.vector.memset(f1[:].bitcast(I32), 0)
        f2 = sb.tile([P, POOL], F32, name="f2")
        nc.vector.memset(f2[:].bitcast(I32), 0)

        l2 = load_list(offs2, "l2")
        n_words = sb.tile([P, 2 * POOL], U8, name="n_words", align_bytes=64)
        nc.sync.dma_start(n_words[:].bitcast(I32), notes_words[0].bitcast(I32))
        load_plane([nc.sync] * 4, n_scale, notes_scales)
        l3 = load_list(offs3, "l3")
        u_words = sb.tile([P, POOL], U32, name="u_words", align_bytes=64)
        nc.sync.dma_start(u_words[:].bitcast(I32), users_words[0].rearrange("p n t -> p (n t)").bitcast(I32))
        load_plane([nc.sync] * 4, u_scale, users_scales)
        l4 = load_list(offs4, "l4")
        l5 = load_list(offs5, "l5")
        l6 = load_list(offs6, "l6")

        q_bf = sb.tile([P, Q, PACK], BF16, name="q_bf", tag="late_zero", align_bytes=64)
        q_codes = sb.tile([P, Q], U32, name="q_codes", align_bytes=64)
        q_scale = sb.tile([P, Q], U8, name="q_scale", align_bytes=64)
        for h in range(2):
            s = slice(64 * h, 64 * h + 64)
            nc.vector.tensor_copy(out=q_bf[:, s, :].rearrange("p (c i) t -> p c t i", i=4),
                                  in_=q_raw[:, :, s].rearrange("p t (c i) -> p c t i", i=4))
        for h in range(2):
            s = slice(64 * h, 64 * h + 64)
            nc.vector.quantize_mx(out=q_codes[:, s].bitcast(FP8X4), scales=q_scale[:, s],
                                  in_=q_bf[:, s, :].rearrange("p q t -> p (q t)"))
        f3 = sb.tile([P, POOL], F32, name="f3", tag="late_zero", align_bytes=64)
        nc.vector.memset(f3[:].bitcast(I32), 0)

        def scores(name, words, scales):
            acc = ps.tile([P, scales.shape[1]], F32, name=name)
            nc.tensor.matmul_mx(out=acc[:], lhsT=q_codes[:].bitcast(FP8X4), lhsT_scale=q_scale[:],
                                rhs=words, rhs_scale=scales, start=True, stop=True)
            return acc

        a_sb = sb.tile([P, POOL], F32, name="a_sb")
        a0 = scores("a0", k_words[0][:].bitcast(FP8X4), k_scale[:, 0:512])
        a1 = scores("a1", k_words[1][:, 0:256].bitcast(FP8X4), k_scale[:, 512:768])
        a2 = scores("a2", k_words[1][:, 256:384].bitcast(FP8X4), k_scale[:, 768:896])
        a3 = scores("a3", k_words[1][:, 384:512].bitcast(FP8X4), k_scale[:, 896:1024])
        nc.scalar.activation(a_sb[:, 0:512], a0[:], COPY)
        nc.vector.tensor_copy(a_sb[:, 512:768], a1[:])
        nc.vector.tensor_copy(a_sb[:, 768:896], a2[:])
        nc.scalar.activation(a_sb[:, 896:1024], a3[:], COPY)
        b = [scores("b%d" % h, n_words[:, h * 2 * BANK:(h + 1) * 2 * BANK].bitcast(FP4X4),
                    n_scale[:, h * BANK:(h + 1) * BANK]) for h in range(2)]
        c = [scores("c%d" % h, u_words[:, h * BANK:(h + 1) * BANK].bitcast(FP8X4),
                    u_scale[:, h * BANK:(h + 1) * BANK]) for h in range(2)]

        g = sb.tile([P, SLOTS], F32, name="g")
        nc.vector.tensor_copy(g[:, cols(0)], a_sb[:].indirect(half(l1, 0)))
        nc.scalar.activation(g[:, cols(1)], a_sb[:].indirect(half(l1, 1)), COPY)
        nc.vector.tensor_copy(f1[:].indirect(l2[:]), g[:])
        nc.vector.tensor_copy(f2[:].indirect(l3[:]), g[:])

        bb = sb.tile([P, POOL], F32, name="bb", tag="bb_then_gc")
        cc = sb.tile([P, POOL], F32, name="cc")
        b_sb = sb.tile([P, POOL], F32, name="b_sb")
        for h in range(2):
            nc.scalar.copy(b_sb[:, h * BANK:(h + 1) * BANK], b[h][:])
        nc.gpsimd.tensor_tensor(bb[:], b_sb[:], f1[:], ALU.add)
        for h in range(2):
            s = slice(h * BANK, (h + 1) * BANK)
            nc.vector.tensor_tensor(cc[:, s], c[h][:], f2[:, s], ALU.subtract)
        gb = sb.tile([P, SLOTS], F32, name="gb")
        w = sb.tile([P, SLOTS], F32, name="w")
        nc.scalar.activation(gb[:], bb[:].indirect(l4[:]), COPY)
        gc = [sb.tile([P, HALF], F32, name="gc0"), sb.tile([P, HALF], F32, name="gc1", tag="bb_then_gc")]
        nc.vector.tensor_copy(gc[0][:], cc[:].indirect(half(l5, 0)))
        nc.scalar.activation(gc[1][:], cc[:].indirect(half(l5, 1)), COPY)
        for h in range(2):
            nc.vector.tensor_tensor(w[:, cols(h)], gb[:, cols(h)], gc[h][:], ALU.min)
        nc.vector.tensor_copy(f3[:].indirect(l6[:]), w[:])

        aa = sb.tile([P, POOL], F32, name="aa")
        nc.vector.tensor_tensor(aa[:], a_sb[:], f3[:], ALU.subtract)
        y = sb.tile([P, SLOTS], F32, name="y")
        for h in range(2):
            nc.vector.tensor_tensor(y[:, cols(h)], aa[:].indirect(half(l1, h)), w[:, cols(h)], ALU.add)
            nc.sync.dma_start(out[:, cols(h)], y[:, cols(h)])
